import numpy as np, ml_dtypes
CORES = [0,2,5]
N = 3
def setup_inputs(rng):
    return {"x": rng.standard_normal((N, 128, 32), dtype=np.float32).astype(ml_dtypes.bfloat16)}
def reference(x):
    g = np.concatenate(list(x), axis=1)
    return {"y": np.broadcast_to(g, (N,) + g.shape)}

from concourse.bass import DstId, RemoteDMATransfer

W = 32
ENGINES = 16

SCRATCH = {
    "gath": ("sbuf", [128, 96], "bfloat16"),
}
SEMAPHORES = ["local", "sent", "arrived"]


def rank_program(g, core, T, topo):
    rank = T.rank_of(core)
    if rank is None:
        return
    peers = [c for c in T.cores if c != core]
    mine = T.gath[:, rank * W:(rank + 1) * W]

    g.dma_start(mine, T.x[:]).then_inc(T.sem.local, 16)
    g.wait_ge(T.sem.local, 16)

    ids = [DstId(rid=topo.addr(p)[0], pnc=topo.addr(p)[1]) for p in peers]
    g.remote_dma_fused(
        [RemoteDMATransfer(dst_ids=ids, dma_engine_mask=topo.mask(core, peers[0]), remote_sem=T.sem.arrived,
                           srcs=[mine], dsts=[mine for p in peers], alu_op=0)],
        local_sem=T.sem.sent,
    )

    g.wait_ge(T.sem.arrived, ENGINES * len(peers))
    g.dma_start(T.y[:], T.gath[:]).then_inc(T.sem.local, 16)
    g.wait_ge(T.sem.sent, ENGINES)
    g.wait_ge(T.sem.local, 32)
